import numpy as np, ml_dtypes
CORES = [65,73,81,89,97,105,113,121]
N = 8
import mx_ref
NC, WB = 256, 1
D = 2 * WB + 1
BF = ml_dtypes.bfloat16
def setup_inputs(rng):
    def f(*shape):
        return mx_ref.flush((rng.standard_normal(shape, dtype=np.float32) * np.exp2(rng.integers(-2, 3, shape[:-1] + (1,)))).astype(BF))
    return {"w": f(N, 128, D * 512), "x": f(N, 128, 4 * NC)}
def setup_inputs_blocks(rng):
    d = setup_inputs(rng)
    for k in ("w", "x"): d[k] = mx_ref.spread(d[k], rng, 1)
    return d
def setup_inputs_wide(rng):
    d = setup_inputs(rng)
    for k in ("w", "x"): d[k] = mx_ref.flush((d[k].astype(np.float32) * np.exp2(rng.integers(-8, 9, (N, 1, 1))).astype(np.float32)).astype(BF))
    return d
def setup_inputs_zeros(rng):
    d = setup_inputs(rng); v = d["x"].reshape(N, 128, -1, 4).copy()
    v[np.broadcast_to((rng.random((N, 1, v.shape[2], 1)) < 0.33), v.shape)] = 0
    d["x"] = v.reshape(d["x"].shape)
    return d
def reference(w, x):
    QX = [mx_ref.quantize(x[j]) for j in range(N)]
    y = np.zeros((N, 128, NC), np.float32)
    for r in range(N):
        for i in range(D):
            p = mx_ref.matmul(mx_ref.quantize(w[r][:, 512 * i:512 * i + 512]), QX[(r + i - WB) % N])
            y[r] = p if i == 0 else y[r] + p
    return {"y": y}

@@ -1,0 +1,136 @@
+from concourse.bass import DstId, RemoteDMATransfer
+from concourse.mybir import dt, ActivationFunctionType
+
+NCOL = 256
+HALF = NCOL // 2
+WCOL = 128
+
+SCRATCH = {
+    "xb": ("sbuf", [128, 4 * NCOL], "bfloat16"),
+    "wb": ("sbuf", [128, 12 * WCOL], "bfloat16"),
+    "xq": ("sbuf", [128, NCOL], "float8_e4m3fn_x4"),
+    "xs": ("sbuf", [128, NCOL], "uint8"),
+    "wq": ("sbuf", [128, 3 * WCOL], "float8_e4m3fn_x4"),
+    "ws": ("sbuf", [128, 3 * WCOL], "uint8"),
+    "q0": ("sbuf", [128, NCOL], "float8_e4m3fn_x4"),
+    "s0": ("sbuf", [128, NCOL], "uint8"),
+    "q2": ("sbuf", [128, NCOL], "float8_e4m3fn_x4"),
+    "s2": ("sbuf", [128, NCOL], "uint8"),
+    "acc": ("psum", [128, 1024], "float32"),
+    "yb": ("sbuf", [128, NCOL], "float32"),
+}
+SEMAPHORES = ["xl", "wl1", "wl2", "xqd", "wq1", "wq2", "sent", "got", "fwd", "in0", "in2", "mm0", "mm1", "cp", "st"]
+
+
+def _engines(mask):
+    return bin(mask).count("1")
+
+
+def _plan(T, topo):
+    cores = list(T.cores)
+    n = len(cores)
+    every = range(topo.CHIPS * topo.CORES_PER_CHIP)
+    sends, jobs = {}, {}
+    for r, c in enumerate(cores):
+        nb = [(cores[(r + 1) % n], 0), (cores[(r - 1) % n], 2)]
+        mate = [t for t in nb if topo.mates(topo.chip(c), topo.chip(t[0]))][0]
+        far = [t for t in nb if t is not mate][0]
+        own = [p for p in every if topo.chip(p) == topo.chip(c) and p not in cores
+               and topo.may_write(p, mate[0]) and topo.may_write(p, far[0])]
+        same = [p for p in own if topo.die(p) == topo.die(c)]
+        other = [p for p in own if topo.die(p) != topo.die(c)]
+        order = [("q", same[0], far), ("q", other[0], mate), ("s", other[1], far), ("s", same[1], mate)]
+        sends[c] = [(kind, p) for kind, p, _ in order]
+        for kind, p, (dst, sl) in order:
+            jobs[p] = (kind, c, dst, sl)
+    return sends, jobs
+
+
+def _view(T, kind, name):
+    return T[name][:].bitcast(dt.uint8) if kind == "q" else T[name][:]
+
+
+def _write(g, T, topo, src, dst, out_ap, in_ap, remote_sem, local_sem):
+    rid, pid, _ = topo.addr(dst)
+    m = topo.mask(src, dst)
+    g.remote_dma(out_ap=out_ap, in_ap=in_ap, remote_sem=remote_sem, local_sem=local_sem, pid=pid, routing_id=rid,
+                 dma_engine_mask=m)
+    return _engines(m)
+
+
+def rank_program(g, core, T, topo):
+    sends, jobs = _plan(T, topo)
+    S = T.sem
+
+    if core in jobs:
+        kind, src, dst, sl = jobs[core]
+        g.wait_ge(S.got, _engines(topo.mask(src, core)))
+        k = _write(g, T, topo, core, dst, _view(T, kind, "%s%d" % (kind, sl)), _view(T, kind, "x" + kind),
+                   S["in%d" % sl], S.fwd)
+        g.wait_ge(S.fwd, k)
+        return
+
+    rank = T.rank_of(core)
+    if rank is None:
+        return
+    n = len(T.cores)
+    left = T.cores[(rank - 1) % n]
+    first, last = (0, 2) if topo.mates(topo.chip(left), topo.chip(core)) else (2, 0)
+    lo = min(first, 1)
+
+    g.sync.dma_start(T.xb[:], T.x[:]).then_inc(S.xl, 16)
+    g.sync.dma_start(T.wb[:, 512 * lo:512 * lo + 1024], T.w[:, 512 * lo:512 * lo + 1024]).then_inc(S.wl1, 16)
+
+    g.vector.wait_ge(S.xl, 16)
+    g.vector.quantize_mx(T.xq[:], T.xs[:], T.xb[:]).then_inc(S.xqd, 1)
+
+    def quant_w(i, sem):
+        g.vector.quantize_mx(T.wq[:, WCOL * i:WCOL * (i + 1)], T.ws[:, WCOL * i:WCOL * (i + 1)],
+                             T.wb[:, 512 * i:512 * (i + 1)]).then_inc(sem, 1)
+
+    g.vector.wait_ge(S.wl1, 16)
+    quant_w(1, S.wq1)
+    quant_w(first, S.wq1)
+
+    g.wait_ge(S.xqd, 1)
+    left_core = 0
+    for kind, p in sends[core]:
+        left_core += _write(g, T, topo, core, p, _view(T, kind, "x" + kind), _view(T, kind, "x" + kind), S.got, S.sent)
+
+    g.sync.wait_ge(S.sent, left_core)
+    g.sync.dma_start(T.wb[:, 512 * last:512 * last + 512], T.w[:, 512 * last:512 * last + 512]).then_inc(S.wl2, 16)
+    g.vector.wait_ge(S.wl2, 16)
+    quant_w(last, S.wq2)
+
+    def slice_mm(i, q, s, start, stop):
+        out = []
+        for h in range(2):
+            out.append(g.tensor.matmul_mx(T.acc[:, 512 * h:512 * h + HALF],
+                                          T.wq[:, WCOL * i:WCOL * (i + 1)], T.ws[:, WCOL * i:WCOL * (i + 1)],
+                                          T[q][:, HALF * h:HALF * (h + 1)], T[s][:, HALF * h:HALF * (h + 1)],
+                                          start, stop))
+        return out
+
+    per_tile = 2 * _engines(topo.mask(jobs_src(jobs, core), core))
+    g.tensor.wait_ge(S.xqd, 1)
+    g.tensor.wait_ge(S.wq1, 2)
+    slice_mm(1, "xq", "xs", True, False)
+    g.tensor.wait_ge(S["in%d" % first], per_tile)
+    slice_mm(first, "q%d" % first, "s%d" % first, False, False)
+    g.tensor.wait_ge(S.wq2, 1)
+    g.tensor.wait_ge(S["in%d" % last], per_tile)
+    a, b = slice_mm(last, "q%d" % last, "s%d" % last, False, True)
+    a.then_inc(S.mm0, 1)
+    b.then_inc(S.mm1, 1)
+
+    g.vector.wait_ge(S.mm0, 1)
+    g.vector.tensor_copy(T.yb[:, 0:HALF], T.acc[:, 0:HALF]).then_inc(S.cp, 1)
+    g.scalar.wait_ge(S.mm1, 1)
+    g.scalar.activation(T.yb[:, HALF:NCOL], T.acc[:, 512:512 + HALF], ActivationFunctionType.Copy).then_inc(S.cp, 1)
+    g.sync.wait_ge(S.cp, 2)
+    g.sync.dma_start(T.y[:], T.yb[:]).then_inc(S.st, 16)
+    g.sync.wait_ge(S.st, 16)
+
+
+def jobs_src(jobs, core):
+    return [p for p, j in jobs.items() if j[2] == core][0]

@@ -19,7 +19,8 @@ SCRATCH = {
     "acc": ("psum", [128, 1024], "float32"),
     "yb": ("sbuf", [128, NCOL], "float32"),
 }
-SEMAPHORES = ["xl", "wl1", "wl2", "xqd", "wq1", "wq2", "sent", "got", "fwd", "in0", "in2", "mm0", "mm1", "cp", "st"]
+SEMAPHORES = ["xl0", "xl1", "wl", "xd0", "xd1", "wd", "sent", "got0", "got1", "fwd",
+              "in00", "in01", "in20", "in21", "mm0", "mm1", "cp0", "cp1", "st"]
 
 
 def _engines(mask):
@@ -39,23 +40,19 @@ def _plan(T, topo):
                and topo.may_write(p, mate[0]) and topo.may_write(p, far[0])]
         same = [p for p in own if topo.die(p) == topo.die(c)]
         other = [p for p in own if topo.die(p) != topo.die(c)]
-        order = [("q", same[0], far), ("q", other[0], mate), ("s", other[1], far), ("s", same[1], mate)]
-        sends[c] = [(kind, p) for kind, p, _ in order]
-        for kind, p, (dst, sl) in order:
-            jobs[p] = (kind, c, dst, sl)
+        r1 = [same[0], other[1]]
+        r2 = [other[0], same[1]]
+        sends[c] = [("q", 0, r1), ("s", 0, r2), ("q", 1, r2), ("s", 1, r1)]
+        for p, (dst, sl) in zip(r1, (far, mate)):
+            jobs[p] = (c, dst, sl, [("q", 0), ("s", 1)])
+        for p, (dst, sl) in zip(r2, (far, mate)):
+            jobs[p] = (c, dst, sl, [("s", 0), ("q", 1)])
     return sends, jobs
 
 
-def _view(T, kind, name):
-    return T[name][:].bitcast(dt.uint8) if kind == "q" else T[name][:]
-
-
-def _write(g, T, topo, src, dst, out_ap, in_ap, remote_sem, local_sem):
-    rid, pid, _ = topo.addr(dst)
-    m = topo.mask(src, dst)
-    g.remote_dma(out_ap=out_ap, in_ap=in_ap, remote_sem=remote_sem, local_sem=local_sem, pid=pid, routing_id=rid,
-                 dma_engine_mask=m)
-    return _engines(m)
+def _view(T, kind, name, h):
+    v = T[name][:, HALF * h:HALF * (h + 1)]
+    return v.bitcast(dt.uint8) if kind == "q" else v
 
 
 def rank_program(g, core, T, topo):
@@ -63,11 +60,15 @@ def rank_program(g, core, T, topo):
     S = T.sem
 
     if core in jobs:
-        kind, src, dst, sl = jobs[core]
-        g.wait_ge(S.got, _engines(topo.mask(src, core)))
-        k = _write(g, T, topo, core, dst, _view(T, kind, "%s%d" % (kind, sl)), _view(T, kind, "x" + kind),
-                   S["in%d" % sl], S.fwd)
-        g.wait_ge(S.fwd, k)
+        src, dst, sl, parts = jobs[core]
+        rid, pid, _ = topo.addr(dst)
+        m = topo.mask(core, dst)
+        for kind, h in parts:
+            g.wait_ge(S["got%d" % h], _engines(topo.mask(src, core)))
+            g.remote_dma(out_ap=_view(T, kind, "%s%d" % (kind, sl), h), in_ap=_view(T, kind, "x" + kind, h),
+                         remote_sem=S["in%d%d" % (sl, h)], local_sem=S.fwd, pid=pid, routing_id=rid,
+                         dma_engine_mask=m)
+        g.wait_ge(S.fwd, len(parts) * _engines(m))
         return
 
     rank = T.rank_of(core)
@@ -76,61 +77,53 @@ def rank_program(g, core, T, topo):
     n = len(T.cores)
     left = T.cores[(rank - 1) % n]
     first, last = (0, 2) if topo.mates(topo.chip(left), topo.chip(core)) else (2, 0)
-    lo = min(first, 1)
 
-    g.sync.dma_start(T.xb[:], T.x[:]).then_inc(S.xl, 16)
-    g.sync.dma_start(T.wb[:, 512 * lo:512 * lo + 1024], T.w[:, 512 * lo:512 * lo + 1024]).then_inc(S.wl1, 16)
+    for h in range(2):
+        g.sync.dma_start(T.xb[:, 512 * h:512 * (h + 1)], T.x[:, 512 * h:512 * (h + 1)]).then_inc(S["xl%d" % h], 16)
+    g.sync.dma_start(T.wb[:], T.w[:]).then_inc(S.wl, 16)
 
-    g.vector.wait_ge(S.xl, 16)
-    g.vector.quantize_mx(T.xq[:], T.xs[:], T.xb[:]).then_inc(S.xqd, 1)
-
-    def quant_w(i, sem):
+    for h in range(2):
+        g.vector.wait_ge(S["xl%d" % h], 16)
+        g.vector.quantize_mx(T.xq[:, HALF * h:HALF * (h + 1)], T.xs[:, HALF * h:HALF * (h + 1)],
+                             T.xb[:, 512 * h:512 * (h + 1)]).then_inc(S["xd%d" % h], 1)
+    g.vector.wait_ge(S.wl, 16)
+    for i in (1, first, last):
         g.vector.quantize_mx(T.wq[:, WCOL * i:WCOL * (i + 1)], T.ws[:, WCOL * i:WCOL * (i + 1)],
-                             T.wb[:, 512 * i:512 * (i + 1)]).then_inc(sem, 1)
+                             T.wb[:, 512 * i:512 * (i + 1)]).then_inc(S.wd, 1)
 
-    g.vector.wait_ge(S.wl1, 16)
-    quant_w(1, S.wq1)
-    quant_w(first, S.wq1)
+    gone = 0
+    for kind, h, relays in sends[core]:
+        g.wait_ge(S["xd%d" % h], 1)
+        m = topo.mask(core, relays[0]) & topo.mask(core, relays[1])
+        v = _view(T, kind, "x" + kind, h)
+        ids = [DstId(rid=topo.addr(p)[0], pnc=topo.addr(p)[1]) for p in relays]
+        g.remote_dma_fused([RemoteDMATransfer(dst_ids=ids, dma_engine_mask=m, remote_sem=S["got%d" % h],
+                                              srcs=[v], dsts=[v for _ in relays])], local_sem=S.sent)
+        gone += _engines(m)
+    g.wait_ge(S.sent, gone)
 
-    g.wait_ge(S.xqd, 1)
-    left_core = 0
-    for kind, p in sends[core]:
-        left_core += _write(g, T, topo, core, p, _view(T, kind, "x" + kind), _view(T, kind, "x" + kind), S.got, S.sent)
+    def mm(i, h, q, s, start, stop):
+        return g.tensor.matmul_mx(T.acc[:, 512 * h:512 * h + HALF],
+                                  T.wq[:, WCOL * i:WCOL * (i + 1)], T.ws[:, WCOL * i:WCOL * (i + 1)],
+                                  T[q][:, HALF * h:HALF * (h + 1)], T[s][:, HALF * h:HALF * (h + 1)], start, stop)
 
-    g.sync.wait_ge(S.sent, left_core)
-    g.sync.dma_start(T.wb[:, 512 * last:512 * last + 512], T.w[:, 512 * last:512 * last + 512]).then_inc(S.wl2, 16)
-    g.vector.wait_ge(S.wl2, 16)
-    quant_w(last, S.wq2)
-
-    def slice_mm(i, q, s, start, stop):
-        out = []
-        for h in range(2):
-            out.append(g.tensor.matmul_mx(T.acc[:, 512 * h:512 * h + HALF],
-                                          T.wq[:, WCOL * i:WCOL * (i + 1)], T.ws[:, WCOL * i:WCOL * (i + 1)],
-                                          T[q][:, HALF * h:HALF * (h + 1)], T[s][:, HALF * h:HALF * (h + 1)],
-                                          start, stop))
-        return out
-
-    per_tile = 2 * _engines(topo.mask(jobs_src(jobs, core), core))
-    g.tensor.wait_ge(S.xqd, 1)
-    g.tensor.wait_ge(S.wq1, 2)
-    slice_mm(1, "xq", "xs", True, False)
-    g.tensor.wait_ge(S["in%d" % first], per_tile)
-    slice_mm(first, "q%d" % first, "s%d" % first, False, False)
-    g.tensor.wait_ge(S.wq2, 1)
-    g.tensor.wait_ge(S["in%d" % last], per_tile)
-    a, b = slice_mm(last, "q%d" % last, "s%d" % last, False, True)
-    a.then_inc(S.mm0, 1)
-    b.then_inc(S.mm1, 1)
+    lands = {sl: sum(_engines(topo.mask(p, core)) for p, j in jobs.items() if j[1] == core and j[2] == sl)
+             for sl in (0, 2)}
+    g.tensor.wait_ge(S.wd, 3)
+    for h in range(2):
+        g.tensor.wait_ge(S["xd%d" % h], 1)
+        mm(1, h, "xq", "xs", True, False)
+    for h in range(2):
+        g.tensor.wait_ge(S["in%d%d" % (first, h)], lands[first])
+        mm(first, h, "q%d" % first, "s%d" % first, False, False)
+        g.tensor.wait_ge(S["in%d%d" % (last, h)], lands[last])
+        mm(last, h, "q%d" % last, "s%d" % last, False, True).then_inc(S["mm%d" % h], 1)
 
     g.vector.wait_ge(S.mm0, 1)
-    g.vector.tensor_copy(T.yb[:, 0:HALF], T.acc[:, 0:HALF]).then_inc(S.cp, 1)
+    g.vector.tensor_copy(T.yb[:, 0:HALF], T.acc[:, 0:HALF]).then_inc(S.cp0, 1)
     g.scalar.wait_ge(S.mm1, 1)
-    g.scalar.activation(T.yb[:, HALF:NCOL], T.acc[:, 512:512 + HALF], ActivationFunctionType.Copy).then_inc(S.cp, 1)
-    g.sync.wait_ge(S.cp, 2)
-    g.sync.dma_start(T.y[:], T.yb[:]).then_inc(S.st, 16)
-    g.sync.wait_ge(S.st, 16)
-
-
-def jobs_src(jobs, core):
-    return [p for p, j in jobs.items() if j[2] == core][0]
+    g.scalar.activation(T.yb[:, HALF:NCOL], T.acc[:, 512:512 + HALF], ActivationFunctionType.Copy).then_inc(S.cp1, 1)
+    for h in range(2):
+        g.sync.wait_ge(S["cp%d" % h], 1)
+        g.sync.dma_start(T.y[:, HALF * h:HALF * (h + 1)], T.yb[:, HALF * h:HALF * (h + 1)]).then_inc(S.st, 16)
+    g.sync.wait_ge(S.st, 32)

@@ -1,4 +1,3 @@
-from concourse.bass import DstId, RemoteDMATransfer
 from concourse.mybir import dt, ActivationFunctionType
 
 NCOL = 256
@@ -19,12 +18,18 @@ SCRATCH = {
     "acc": ("psum", [128, 1024], "float32"),
     "yb": ("sbuf", [128, NCOL], "float32"),
 }
-SEMAPHORES = ["xl0", "xl1", "wl", "xd0", "xd1", "wd", "sent", "got0", "got1", "fwd",
+SEMAPHORES = ["xl0", "xl1", "wl0", "wl1", "xd0", "xd1", "wd0", "wd1", "sents", "sentq", "gots", "gotq", "fwd",
               "in00", "in01", "in20", "in21", "mm0", "mm1", "cp0", "cp1", "st"]
 
 
 def _engines(mask):
     return bin(mask).count("1")
+
+
+def _part(mask, parts, i):
+    bits = [b for b in range(mask.bit_length()) if (mask >> b) & 1]
+    k = len(bits) // parts
+    return sum(1 << b for b in bits[k * i:k * (i + 1)])
 
 
 def _plan(T, topo):
@@ -40,13 +45,16 @@ def _plan(T, topo):
                and topo.may_write(p, mate[0]) and topo.may_write(p, far[0])]
         same = [p for p in own if topo.die(p) == topo.die(c)]
         other = [p for p in own if topo.die(p) != topo.die(c)]
-        r1 = [same[0], other[1]]
-        r2 = [other[0], same[1]]
-        sends[c] = [("q", 0, r1), ("s", 0, r2), ("q", 1, r2), ("s", 1, r1)]
-        for p, (dst, sl) in zip(r1, (far, mate)):
-            jobs[p] = (c, dst, sl, [("q", 0), ("s", 1)])
-        for p, (dst, sl) in zip(r2, (far, mate)):
-            jobs[p] = (c, dst, sl, [("s", 0), ("q", 1)])
+        teams = [((other[0], same[0]), far), ((same[1], other[1]), mate)]
+        sends[c] = []
+        for kind in ("s", "q"):
+            for d, (team, (dst, sl)) in enumerate(teams):
+                for h, p in enumerate(team):
+                    m = topo.mask(c, p)
+                    if kind == "s":
+                        m = _part(m, 2, 1 if (d, h) == (1, 1) else 0)
+                    sends[c].append((kind, h, p, m))
+                    jobs.setdefault(p, (dst, sl, h, {}))[3][kind] = _engines(m)
     return sends, jobs
 
 
@@ -60,15 +68,15 @@ def rank_program(g, core, T, topo):
     S = T.sem
 
     if core in jobs:
-        src, dst, sl, parts = jobs[core]
+        dst, sl, h, k_in = jobs[core]
         rid, pid, _ = topo.addr(dst)
         m = topo.mask(core, dst)
-        for kind, h in parts:
-            g.wait_ge(S["got%d" % h], _engines(topo.mask(src, core)))
+        for kind in ("s", "q"):
+            g.wait_ge(S["got" + kind], k_in[kind])
             g.remote_dma(out_ap=_view(T, kind, "%s%d" % (kind, sl), h), in_ap=_view(T, kind, "x" + kind, h),
                          remote_sem=S["in%d%d" % (sl, h)], local_sem=S.fwd, pid=pid, routing_id=rid,
                          dma_engine_mask=m)
-        g.wait_ge(S.fwd, len(parts) * _engines(m))
+        g.wait_ge(S.fwd, 2 * _engines(m))
         return
 
     rank = T.rank_of(core)
@@ -78,45 +86,55 @@ def rank_program(g, core, T, topo):
     left = T.cores[(rank - 1) % n]
     first, last = (0, 2) if topo.mates(topo.chip(left), topo.chip(core)) else (2, 0)
 
+    def load_w(i, sem):
+        g.sync.dma_start(T.wb[:, 512 * i:512 * (i + 1)], T.w[:, 512 * i:512 * (i + 1)]).then_inc(sem, 16)
+
+    def quant_w(i, sem):
+        g.vector.quantize_mx(T.wq[:, WCOL * i:WCOL * (i + 1)], T.ws[:, WCOL * i:WCOL * (i + 1)],
+                             T.wb[:, 512 * i:512 * (i + 1)]).then_inc(sem, 1)
+
     for h in range(2):
         g.sync.dma_start(T.xb[:, 512 * h:512 * (h + 1)], T.x[:, 512 * h:512 * (h + 1)]).then_inc(S["xl%d" % h], 16)
-    g.sync.dma_start(T.wb[:], T.w[:]).then_inc(S.wl, 16)
+    load_w(1, S.wl0)
 
     for h in range(2):
         g.vector.wait_ge(S["xl%d" % h], 16)
         g.vector.quantize_mx(T.xq[:, HALF * h:HALF * (h + 1)], T.xs[:, HALF * h:HALF * (h + 1)],
                              T.xb[:, 512 * h:512 * (h + 1)]).then_inc(S["xd%d" % h], 1)
-    g.vector.wait_ge(S.wl, 16)
-    for i in (1, first, last):
-        g.vector.quantize_mx(T.wq[:, WCOL * i:WCOL * (i + 1)], T.ws[:, WCOL * i:WCOL * (i + 1)],
-                             T.wb[:, 512 * i:512 * (i + 1)]).then_inc(S.wd, 1)
+    g.vector.wait_ge(S.wl0, 16)
+    quant_w(1, S.wd0)
 
-    gone = 0
-    for kind, h, relays in sends[core]:
+    gone = {"s": 0, "q": 0}
+    for kind, h, p, m in sends[core]:
         g.wait_ge(S["xd%d" % h], 1)
-        m = topo.mask(core, relays[0]) & topo.mask(core, relays[1])
         v = _view(T, kind, "x" + kind, h)
-        ids = [DstId(rid=topo.addr(p)[0], pnc=topo.addr(p)[1]) for p in relays]
-        g.remote_dma_fused([RemoteDMATransfer(dst_ids=ids, dma_engine_mask=m, remote_sem=S["got%d" % h],
-                                              srcs=[v], dsts=[v for _ in relays])], local_sem=S.sent)
-        gone += _engines(m)
-    g.wait_ge(S.sent, gone)
+        g.remote_dma(out_ap=v, in_ap=v, remote_sem=S["got" + kind], local_sem=S["sent" + kind], pid=topo.addr(p)[1],
+                     routing_id=topo.addr(p)[0], dma_engine_mask=m)
+        gone[kind] += _engines(m)
+    g.wait_ge(S.sentq, gone["q"])
+
+    g.sync.wait_ge(S.sents, gone["s"])
+    load_w(first, S.wl1)
+    load_w(last, S.wl1)
+    g.vector.wait_ge(S.wl1, 32)
+    quant_w(first, S.wd1)
+    quant_w(last, S.wd1)
 
     def mm(i, h, q, s, start, stop):
         return g.tensor.matmul_mx(T.acc[:, 512 * h:512 * h + HALF],
                                   T.wq[:, WCOL * i:WCOL * (i + 1)], T.ws[:, WCOL * i:WCOL * (i + 1)],
                                   T[q][:, HALF * h:HALF * (h + 1)], T[s][:, HALF * h:HALF * (h + 1)], start, stop)
 
-    lands = {sl: sum(_engines(topo.mask(p, core)) for p, j in jobs.items() if j[1] == core and j[2] == sl)
-             for sl in (0, 2)}
-    g.tensor.wait_ge(S.wd, 3)
+    lands = {(j[1], j[2]): 2 * _engines(topo.mask(p, core)) for p, j in jobs.items() if j[0] == core}
+    g.tensor.wait_ge(S.wd0, 1)
     for h in range(2):
         g.tensor.wait_ge(S["xd%d" % h], 1)
         mm(1, h, "xq", "xs", True, False)
+    g.tensor.wait_ge(S.wd1, 2)
     for h in range(2):
-        g.tensor.wait_ge(S["in%d%d" % (first, h)], lands[first])
+        g.tensor.wait_ge(S["in%d%d" % (first, h)], lands[(first, h)])
         mm(first, h, "q%d" % first, "s%d" % first, False, False)
-        g.tensor.wait_ge(S["in%d%d" % (last, h)], lands[last])
+        g.tensor.wait_ge(S["in%d%d" % (last, h)], lands[(last, h)])
         mm(last, h, "q%d" % last, "s%d" % last, False, True).then_inc(S["mm%d" % h], 1)
 
     g.vector.wait_ge(S.mm0, 1)

from concourse.mybir import dt, ActivationFunctionType

NCOL = 256
HALF = NCOL // 2
WCOL = 128

SCRATCH = {
    "xb": ("sbuf", [128, 4 * NCOL], "bfloat16"),
    "wb": ("sbuf", [128, 12 * WCOL], "bfloat16"),
    "xq": ("sbuf", [128, NCOL], "float8_e4m3fn_x4"),
    "xs": ("sbuf", [128, NCOL], "uint8"),
    "wq": ("sbuf", [128, 3 * WCOL], "float8_e4m3fn_x4"),
    "ws": ("sbuf", [128, 3 * WCOL], "uint8"),
    "q0": ("sbuf", [128, NCOL], "float8_e4m3fn_x4"),
    "s0": ("sbuf", [128, NCOL], "uint8"),
    "q2": ("sbuf", [128, NCOL], "float8_e4m3fn_x4"),
    "s2": ("sbuf", [128, NCOL], "uint8"),
    "acc": ("psum", [128, 1024], "float32"),
    "yb": ("sbuf", [128, NCOL], "float32"),
}
SEMAPHORES = ["xl0", "xl1", "wl0", "wl1", "xd0", "xd1", "wd0", "wd1", "sents", "sentq", "gots", "gotq", "fwd",
              "in00", "in01", "in20", "in21", "mm0", "mm1", "cp0", "cp1", "st"]


def _engines(mask):
    return bin(mask).count("1")


def _part(mask, parts, i):
    bits = [b for b in range(mask.bit_length()) if (mask >> b) & 1]
    k = len(bits) // parts
    return sum(1 << b for b in bits[k * i:k * (i + 1)])


def _plan(T, topo):
    cores = list(T.cores)
    n = len(cores)
    every = range(topo.CHIPS * topo.CORES_PER_CHIP)
    sends, jobs = {}, {}
    for r, c in enumerate(cores):
        nb = [(cores[(r + 1) % n], 0), (cores[(r - 1) % n], 2)]
        mate = [t for t in nb if topo.mates(topo.chip(c), topo.chip(t[0]))][0]
        far = [t for t in nb if t is not mate][0]
        own = [p for p in every if topo.chip(p) == topo.chip(c) and p not in cores
               and topo.may_write(p, mate[0]) and topo.may_write(p, far[0])]
        same = [p for p in own if topo.die(p) == topo.die(c)]
        other = [p for p in own if topo.die(p) != topo.die(c)]
        teams = [((other[0], same[0]), far), ((same[1], other[1]), mate)]
        sends[c] = []
        for kind in ("s", "q"):
            for d, (team, (dst, sl)) in enumerate(teams):
                for h, p in enumerate(team):
                    m = topo.mask(c, p)
                    if kind == "s":
                        m = _part(m, 2, 1 if (d, h) == (1, 1) else 0)
                    sends[c].append((kind, h, p, m))
                    jobs.setdefault(p, (dst, sl, h, {}))[3][kind] = _engines(m)
    return sends, jobs


def _view(T, kind, name, h):
    v = T[name][:, HALF * h:HALF * (h + 1)]
    return v.bitcast(dt.uint8) if kind == "q" else v


def rank_program(g, core, T, topo):
    sends, jobs = _plan(T, topo)
    S = T.sem

    if core in jobs:
        dst, sl, h, k_in = jobs[core]
        rid, pid, _ = topo.addr(dst)
        m = topo.mask(core, dst)
        for kind in ("s", "q"):
            g.wait_ge(S["got" + kind], k_in[kind])
            g.remote_dma(out_ap=_view(T, kind, "%s%d" % (kind, sl), h), in_ap=_view(T, kind, "x" + kind, h),
                         remote_sem=S["in%d%d" % (sl, h)], local_sem=S.fwd, pid=pid, routing_id=rid,
                         dma_engine_mask=m)
        g.wait_ge(S.fwd, 2 * _engines(m))
        return

    rank = T.rank_of(core)
    if rank is None:
        return
    n = len(T.cores)
    left = T.cores[(rank - 1) % n]
    first, last = (0, 2) if topo.mates(topo.chip(left), topo.chip(core)) else (2, 0)

    def load_w(i, sem):
        g.sync.dma_start(T.wb[:, 512 * i:512 * (i + 1)], T.w[:, 512 * i:512 * (i + 1)]).then_inc(sem, 16)

    def quant_w(i, sem):
        g.vector.quantize_mx(T.wq[:, WCOL * i:WCOL * (i + 1)], T.ws[:, WCOL * i:WCOL * (i + 1)],
                             T.wb[:, 512 * i:512 * (i + 1)]).then_inc(sem, 1)

    for h in range(2):
        g.sync.dma_start(T.xb[:, 512 * h:512 * (h + 1)], T.x[:, 512 * h:512 * (h + 1)]).then_inc(S["xl%d" % h], 16)
    load_w(1, S.wl0)

    for h in range(2):
        g.vector.wait_ge(S["xl%d" % h], 16)
        g.vector.quantize_mx(T.xq[:, HALF * h:HALF * (h + 1)], T.xs[:, HALF * h:HALF * (h + 1)],
                             T.xb[:, 512 * h:512 * (h + 1)]).then_inc(S["xd%d" % h], 1)
    g.vector.wait_ge(S.wl0, 16)
    quant_w(1, S.wd0)

    gone = {"s": 0, "q": 0}
    for kind, h, p, m in sends[core]:
        g.wait_ge(S["xd%d" % h], 1)
        v = _view(T, kind, "x" + kind, h)
        g.remote_dma(out_ap=v, in_ap=v, remote_sem=S["got" + kind], local_sem=S["sent" + kind], pid=topo.addr(p)[1],
                     routing_id=topo.addr(p)[0], dma_engine_mask=m)
        gone[kind] += _engines(m)
    g.wait_ge(S.sentq, gone["q"])

    g.sync.wait_ge(S.sents, gone["s"])
    load_w(first, S.wl1)
    load_w(last, S.wl1)
    g.vector.wait_ge(S.wl1, 32)
    quant_w(first, S.wd1)
    quant_w(last, S.wd1)

    def mm(i, h, q, s, start, stop):
        return g.tensor.matmul_mx(T.acc[:, 512 * h:512 * h + HALF],
                                  T.wq[:, WCOL * i:WCOL * (i + 1)], T.ws[:, WCOL * i:WCOL * (i + 1)],
                                  T[q][:, HALF * h:HALF * (h + 1)], T[s][:, HALF * h:HALF * (h + 1)], start, stop)

    lands = {(j[1], j[2]): 2 * _engines(topo.mask(p, core)) for p, j in jobs.items() if j[0] == core}
    g.tensor.wait_ge(S.wd0, 1)
    for h in range(2):
        g.tensor.wait_ge(S["xd%d" % h], 1)
        mm(1, h, "xq", "xs", True, False)
    g.tensor.wait_ge(S.wd1, 2)
    for h in range(2):
        g.tensor.wait_ge(S["in%d%d" % (first, h)], lands[(first, h)])
        mm(first, h, "q%d" % first, "s%d" % first, False, False)
        g.tensor.wait_ge(S["in%d%d" % (last, h)], lands[(last, h)])
        mm(last, h, "q%d" % last, "s%d" % last, False, True).then_inc(S["mm%d" % h], 1)

    g.vector.wait_ge(S.mm0, 1)
    g.vector.tensor_copy(T.yb[:, 0:HALF], T.acc[:, 0:HALF]).then_inc(S.cp0, 1)
    g.scalar.wait_ge(S.mm1, 1)
    g.scalar.activation(T.yb[:, HALF:NCOL], T.acc[:, 512:512 + HALF], ActivationFunctionType.Copy).then_inc(S.cp1, 1)
    for h in range(2):
        g.sync.wait_ge(S["cp%d" % h], 1)
        g.sync.dma_start(T.y[:, HALF * h:HALF * (h + 1)], T.yb[:, HALF * h:HALF * (h + 1)]).then_inc(S.st, 16)
    g.sync.wait_ge(S.st, 32)
